import numpy as np
import ml_dtypes


def mxq(x, axis, fmt="e4m3"):
    dtype, down = {"e4m3": (ml_dtypes.float8_e4m3fn, 7), "e5m2": (ml_dtypes.float8_e5m2, 14)}[fmt]
    v = np.moveaxis(np.asarray(x, np.float32).astype(ml_dtypes.bfloat16).astype(np.float64), axis, -1)
    blocks = v.reshape(v.shape[:-1] + (-1, 32))
    amax = np.abs(blocks).max(-1, keepdims=True)
    byte = np.maximum(np.where(amax > 0, np.frexp(amax)[1] - 1 + 127, 0) - down, 1)
    scale = np.exp2(byte - 127.0)
    codes = (blocks / scale).astype(np.float32).astype(dtype).astype(np.float64)
    return np.moveaxis((codes * scale).reshape(v.shape), -1, axis)


WIDE = False


def mx_kscale(k):
    if not WIDE:
        return np.ones(k)
    levels = np.array([10, -10, 5, -5, 0])
    if k % 512:
        return np.exp2(np.random.permutation(np.resize(levels, k // 32))).repeat(32)
    a = np.empty((k // 512, 16))
    for p in range(k // 512):
        a[p, :8] = np.random.permutation(np.resize(levels, 8))
        for g in range(8):
            far = levels[np.abs(levels - a[p, g]) >= 10]
            a[p, g + 8] = far[np.random.randint(len(far))]
    return np.exp2(a.ravel()).repeat(32)


def f64(x):
    return np.asarray(x).astype(np.float64)


def striped(idx):
    return np.tile(idx.reshape(-1, 16).T, (8, 1)).astype(np.uint16)


def unstriped(offs):
    return offs[:16].T.reshape(-1).astype(np.int64)


def pack_weight(w):
    k, n = w.shape
    w = f64(np.asarray(w, np.float32).astype(ml_dtypes.bfloat16)).reshape(k // 32, 32, n)
    amax = np.abs(w).max(1)
    byte = np.clip(np.where(amax > 0, np.frexp(amax)[1] - 1 + 127 - 7, 1), 1, 254)
    scaled = (w * np.exp2(127.0 - byte)[:, None, :]).reshape(k, n).astype(np.float32)
    words = np.ascontiguousarray(scaled.reshape(k // 512, 128, 4, n).transpose(0, 1, 3, 2)).astype(ml_dtypes.float8_e4m3fn).view(np.uint8)
    return words, np.ascontiguousarray(byte.astype(np.uint8).reshape(k // 512, 16, n))


def unpack_weight(words, scales):
    g, p, n, _ = words.shape
    vals = np.ascontiguousarray(words).view(ml_dtypes.float8_e4m3fn).astype(np.float64) * np.repeat(np.exp2(scales.astype(np.float64) - 127.0), 8, axis=1)[..., None]
    return vals.transpose(0, 1, 3, 2).reshape(g * 512, n)


def silu(v):
    return v / (1.0 + np.exp(-np.maximum(v, -700.0)))


K, T, S, H, N = 512, 2048, 1024, 512, 128
P = 2 ** 7


def setup_inputs():
    n = np.random.standard_normal
    s = mx_kscale(K)[:, None]
    u = mx_kscale(H)
    packed_w2 = pack_weight(n((H, N)) / np.sqrt(H) / u[:, None])
    return {
        "xT": (n((K, T)) * s).astype(np.float32),
        "gate": np.tile(np.random.uniform(0.2, 1.0, S), (P, 1)).astype(np.float32),
        "res": n((N, T)).astype(np.float32),
        "w1": (n((K, H)) / np.sqrt(K) / s).astype(np.float32),
        "w3": (n((K, H)) / np.sqrt(K) / s * u).astype(np.float32),
        "w2_words": packed_w2[0],
        "w2_scales": packed_w2[1],
        "offs": striped(np.random.permutation(T)[:S]),
    }


def reference(xT, gate, res, w1, w3, w2_words, w2_scales, offs):
    r = f64(res)[:, unstriped(offs)]
    xq = mxq(f64(xT)[:, unstriped(offs)], 0, "e4m3")
    h = (silu(mxq(f64(w1), 0, "e4m3").T @ xq)) * ((mxq(f64(w3), 0, "e4m3").T @ xq))
    y = unpack_weight(w2_words, w2_scales).T @ mxq(h, 0, "e4m3")
    out = f64(res).copy()
    out[:, unstriped(offs)] = r + y * f64(gate)[:1]
    return out

@@ -1,0 +1,206 @@
+from contextlib import ExitStack
+
+import concourse.mybir as mybir
+from concourse.masks import make_identity
+
+K, T, S, H, N = 512, 2048, 1024, 512, 128
+FLOPS = 2 * K * H * S * 2 + 2 * H * N * S
+BYTES = 4 * (K * T + S + 2 * N * T + 2 * K * H) + H * N + 16 * N + 2 * 128 * (S // 16)
+
+F32 = mybir.dt.float32
+BF16 = mybir.dt.bfloat16
+U32 = mybir.dt.uint32
+U16 = mybir.dt.uint16
+U8 = mybir.dt.uint8
+I32 = mybir.dt.int32
+FP8X4 = mybir.dt.float8_e4m3fn_x4
+ACT = mybir.ActivationFunctionType
+ALU = mybir.AluOpType
+
+P = 128
+PACK = 4
+BLOCK = 128
+GROUP = 512
+
+
+def tile_picked_modres_glusilu_l_kernel(
+    tc, xT, gate, res, w1, w3, w2_words, w2_scales, offs, out
+):
+    nc = tc.nc
+    groups = S // GROUP
+    blocks = S // BLOCK
+
+    with ExitStack() as ctx:
+        keep = ctx.enter_context(tc.tile_pool(name="keep", bufs=1))
+        ring = ctx.enter_context(tc.tile_pool(name="ring", bufs=4))
+        psum = ctx.enter_context(tc.psum_pool(name="psum", bufs=1))
+
+        offsets = keep.tile([P, S // 16], U16, name="offsets")
+        nc.sync.dma_start(offsets[:], offs)
+
+        def entries(g):
+            return offsets[:, g * (GROUP // 16) : (g + 1) * (GROUP // 16)]
+
+        w2_codes = keep.tile([P, N], U32, name="w2_codes", align_bytes=64)
+        w2_plane = keep.tile([P, N], U8, name="w2_plane", align_bytes=64)
+        gate_rows = keep.tile([P, BLOCK], F32, name="gate_rows")
+        identity = keep.tile([P, P], F32, name="identity")
+        warm = keep.tile([P, 2], F32, name="warm")
+        nc.gpsimd.memset(w2_plane[:].bitcast(I32), 0)
+        nc.gpsimd.memset(gate_rows[:], 0.0)
+        nc.gpsimd.memset(warm[:], 0.0)
+        make_identity(nc, identity[:])
+        nc.scalar.dma_start(w2_codes[:].bitcast(I32), w2_words[0].rearrange("p n t -> p (n t)").bitcast(I32))
+        for q in range(4):
+            nc.scalar.dma_start(
+                w2_plane[32 * q : 32 * q + 4, :].bitcast(I32), w2_scales[0, 4 * q : 4 * q + 4, :].bitcast(I32)
+            )
+        nc.scalar.dma_start(gate_rows[0:blocks, :], gate[0:1, :].rearrange("o (c q) -> (o c) q", q=BLOCK))
+        nc.scalar.activation(warm[:, 1:2], warm[:, 0:1], ACT.Silu)
+
+        x_rows = xT.rearrange("(p j) c -> p j c", j=PACK)
+        x_cuts = ([0, 1024, 2048], [0, 512, 1024, 1536, 2048])
+        x_raw = []
+        for u in range(2):
+            for lo, hi in zip(x_cuts[u][:-1], x_cuts[u][1:]):
+                raw = keep.tile([P, 2, hi - lo], F32, name="x_raw_%d_%d" % (u, lo))
+                nc.sync.dma_start(raw[:], x_rows[:, 2 * u : 2 * u + 2, lo:hi])
+                x_raw.append((u, lo, hi, raw))
+        w_raw = []
+        for i, w in enumerate((w1, w3)):
+            for half in range(2):
+                raw = keep.tile([P, PACK, H // 2], F32, name="w_raw_%d_%d" % (i, half))
+                nc.sync.dma_start(
+                    raw[:], w.rearrange("(p j) c -> p j c", j=PACK)[:, :, half * (H // 2) : (half + 1) * (H // 2)]
+                )
+                w_raw.append(raw)
+        window = keep.tile([P, T], F32, name="window")
+        nc.sync.dma_start(window[:], res)
+
+        gate_bank = psum.tile([P, P], F32, name="back", tag="back")
+        nc.tensor.transpose(gate_bank[:], gate_rows[:], identity[:])
+        gate_cols = keep.tile([P, blocks], F32, name="gate_cols")
+        nc.scalar.copy(gate_cols[:], gate_bank[:, 0:blocks])
+
+        pairs = [keep.tile([P, T], U32, name="pairs_%d" % u) for u in range(2)]
+
+        def round_pairs(engine, piece, a, b):
+            u, lo, hi, raw = piece
+            dst = pairs[u][:, lo + a : lo + b].bitcast(BF16).rearrange("p (c e) -> p c e", e=2)
+            src = raw[:, :, a:b].rearrange("p e c -> p c e")
+            if engine is nc.scalar:
+                nc.scalar.copy(dst, src)
+            else:
+                nc.vector.tensor_copy(dst, src)
+
+        picked = [keep.tile([P, GROUP * PACK], BF16, name="picked_%d" % g, align_bytes=64) for g in range(groups)]
+
+        def pick(u, g):
+            words = picked[g][:].bitcast(U32).rearrange("p (n u) -> p n u", u=2)
+            nc.vector.tensor_copy(words[:, :, u], pairs[u][:].indirect(entries(g)))
+
+        def quantize(name, grouped, width, tag=None):
+            codes = keep.tile([P, width], U32, name=name + "_codes", tag=tag or name + "_codes", align_bytes=64)
+            plane = keep.tile([P, width], U8, name=name + "_plane", align_bytes=64)
+            nc.vector.quantize_mx(out=codes[:].bitcast(FP8X4), scales=plane[:], in_=grouped)
+            return codes, plane
+
+        round_pairs(nc.vector, x_raw[0], 0, 1024)
+        round_pairs(nc.vector, x_raw[1], 0, 672)
+        round_pairs(nc.scalar, x_raw[1], 672, 1024)
+        for g in range(groups):
+            pick(0, g)
+        for piece in x_raw[2:5]:
+            round_pairs(nc.scalar, piece, 0, 512)
+        round_pairs(nc.vector, x_raw[5], 0, 352)
+        round_pairs(nc.scalar, x_raw[5], 352, 512)
+
+        w_grouped = [keep.tile([P, H * PACK], BF16, name="w_grouped_%d" % i, tag="w_grouped_%d" % i, align_bytes=64) for i in range(2)]
+
+        def round_weights(engine, i, half):
+            dst = w_grouped[i][:].rearrange("p (t m j) -> p m j t", t=PACK, j=PACK)[:, half * 64 : (half + 1) * 64]
+            src = w_raw[2 * i + half][:].rearrange("p j (m t) -> p m j t", t=PACK)
+            if engine is nc.scalar:
+                nc.scalar.copy(dst, src)
+            else:
+                nc.vector.tensor_copy(dst, src)
+
+        round_weights(nc.scalar, 0, 0)
+        round_weights(nc.scalar, 0, 1)
+        round_weights(nc.scalar, 1, 0)
+        pick(1, 0)
+        pick(1, 1)
+        x_q = [quantize("x_0", picked[0][:], GROUP)]
+        w1_q = quantize("w1", w_grouped[0][:], H)
+        round_weights(nc.vector, 1, 1)
+        w3_q = quantize("w3", w_grouped[1][:], H)
+        x_q.append(quantize("x_1", picked[1][:], GROUP, tag="w_grouped_1"))
+
+        def first_layer(name, w_q, c):
+            bank = psum.tile([P, PACK, BLOCK], F32, name=name, tag=name, bufs=3)
+            codes, plane = x_q[c * BLOCK // GROUP]
+            cols = slice(c * BLOCK % GROUP, c * BLOCK % GROUP + BLOCK)
+            for t in range(PACK):
+                w_cols = slice(t * P, (t + 1) * P)
+                nc.tensor.matmul_mx(
+                    out=bank[:, t, :],
+                    lhsT=w_q[0][:, w_cols].bitcast(FP8X4),
+                    lhsT_scale=w_q[1][:, w_cols],
+                    rhs=codes[:, cols].bitcast(FP8X4),
+                    rhs_scale=plane[:, cols],
+                    start=True,
+                    stop=True,
+                )
+            return bank
+
+        h_grouped = [keep.tile([P, GROUP * PACK], BF16, name="h_grouped_%d" % g, align_bytes=64) for g in range(groups)]
+
+        def hidden(c):
+            a_bank = first_layer("a_bank", w1_q, c)
+            silu_a = ring.tile([P, BLOCK, PACK], F32, name="silu_a")
+            nc.scalar.activation(silu_a[:], a_bank[:].rearrange("p t n -> p n t"), ACT.Silu)
+            b_bank = first_layer("b_bank", w3_q, c)
+            g, first = divmod(c * BLOCK, GROUP)
+            dst = h_grouped[g][:, first * PACK : (first + BLOCK) * PACK].rearrange("p (n t) -> p n t", t=PACK)
+            nc.vector.tensor_tensor(dst, b_bank[:].rearrange("p t n -> p n t"), silu_a[:], ALU.mult)
+
+        gated = [keep.tile([P, GROUP], F32, name="gated_%d" % g) for g in range(groups)]
+
+        def second_layer(g):
+            codes, plane = quantize("h_%d" % g, h_grouped[g][:], GROUP)
+            per = GROUP // BLOCK
+            y_bank = psum.tile([P, per, N], F32, name="y_bank", tag="y_bank")
+            for b in range(per):
+                cols = slice(b * BLOCK, (b + 1) * BLOCK)
+                nc.tensor.matmul_mx(
+                    out=y_bank[:, b, :],
+                    lhsT=codes[:, cols].bitcast(FP8X4),
+                    lhsT_scale=plane[:, cols],
+                    rhs=w2_codes[:].bitcast(FP8X4),
+                    rhs_scale=w2_plane[:],
+                    start=True,
+                    stop=True,
+                )
+            y_tok = ring.tile([P, per, N], F32, name="y_tok")
+            for b in range(per):
+                c = g * per + b
+                nc.scalar.activation(y_tok[:, b, :], y_bank[:, b, :], ACT.Copy, scale=gate_cols[:, c : c + 1])
+            back = psum.tile([P, GROUP], F32, name="back", tag="back")
+            for b in range(per):
+                nc.tensor.transpose(back[:, b * BLOCK : (b + 1) * BLOCK], y_tok[:, b, :], identity[:])
+            nc.scalar.copy(gated[g][:], back[:])
+
+        per = GROUP // BLOCK
+        for c in range(blocks):
+            hidden(c)
+            if c >= per and c % per == 0:
+                second_layer(c // per - 1)
+        second_layer(groups - 1)
+        old = h_grouped[groups - 1][:].bitcast(F32)
+        nc.vector.tensor_copy(old, window[:].indirect(offsets[:]))
+
+        for g in range(groups):
+            nc.vector.tensor_tensor(
+                window[:].indirect(entries(g)), gated[g][:], old[:, g * GROUP : (g + 1) * GROUP], ALU.add
+            )
+        nc.sync.dma_start(out, window[:])

@@ -4,8 +4,8 @@ import concourse.mybir as mybir
 from concourse.masks import make_identity
 
 K, T, S, H, N = 512, 2048, 1024, 512, 128
-FLOPS = 2 * K * H * S * 2 + 2 * H * N * S
-BYTES = 4 * (K * T + S + 2 * N * T + 2 * K * H) + H * N + 16 * N + 2 * 128 * (S // 16)
+FLOPS = 2 * (2 * K * H * S) + 2 * H * N * S
+BYTES = 4 * (K * T + S + 2 * N * T + 2 * K * H) + H * N + (H // 32) * N + 2 * 128 * (S // 16)
 
 F32 = mybir.dt.float32
 BF16 = mybir.dt.bfloat16
@@ -19,188 +19,185 @@ ALU = mybir.AluOpType
 
 P = 128
 PACK = 4
+LANES = 16
 BLOCK = 128
-GROUP = 512
+HALF = 512
+BLOCKS = S // BLOCK
+BLOCKS_PER_HALF = HALF // BLOCK
+GPSIMD_PLACE = 1
+RING = 4
+
+X_LOADS = (
+    ((0, 1024, 0), (1024, 2048, 352)),
+    ((0, 768, 768), (768, 1536, 416), (1536, 2048, 160)),
+)
 
 
 def tile_picked_modres_glusilu_l_kernel(
     tc, xT, gate, res, w1, w3, w2_words, w2_scales, offs, out
 ):
     nc = tc.nc
-    groups = S // GROUP
-    blocks = S // BLOCK
 
     with ExitStack() as ctx:
         keep = ctx.enter_context(tc.tile_pool(name="keep", bufs=1))
-        ring = ctx.enter_context(tc.tile_pool(name="ring", bufs=4))
         psum = ctx.enter_context(tc.psum_pool(name="psum", bufs=1))
 
-        offsets = keep.tile([P, S // 16], U16, name="offsets")
-        nc.sync.dma_start(offsets[:], offs)
+        def copy(engine, dst, src):
+            if engine is nc.scalar:
+                nc.scalar.copy(dst, src)
+            else:
+                nc.vector.tensor_copy(dst, src)
+
+        def quantize(name, values, tag=""):
+            width = values.shape[1] // PACK
+            codes = keep.tile([P, width], U32, name=name + "_codes", tag=tag or name + "_codes", align_bytes=64)
+            scales = keep.tile([P, width], U8, name=name + "_scales", align_bytes=64)
+            nc.vector.quantize_mx(out=codes[:].bitcast(FP8X4), scales=scales[:], in_=values)
+            return codes, scales
+
+        def product(dst, stationary, stationary_cols, moving, moving_cols):
+            nc.tensor.matmul_mx(
+                out=dst,
+                lhsT=stationary[0][:, stationary_cols].bitcast(FP8X4),
+                lhsT_scale=stationary[1][:, stationary_cols],
+                rhs=moving[0][:, moving_cols].bitcast(FP8X4),
+                rhs_scale=moving[1][:, moving_cols],
+                start=True,
+                stop=True,
+            )
+
+        def bank(number, shape):
+            return psum.tile(shape, F32, name="bank_%d" % number, tag="bank_%d" % number)
+
+        offsets = keep.tile([P, S // LANES], U16, name="offsets")
 
         def entries(g):
-            return offsets[:, g * (GROUP // 16) : (g + 1) * (GROUP // 16)]
+            return offsets[:, g * HALF // LANES : (g + 1) * HALF // LANES]
 
-        w2_codes = keep.tile([P, N], U32, name="w2_codes", align_bytes=64)
-        w2_plane = keep.tile([P, N], U8, name="w2_plane", align_bytes=64)
+        w2_code_tile = keep.tile([P, N], U32, name="w2_code_tile", align_bytes=64)
+        w2_scale_tile = keep.tile([P, N], U8, name="w2_scale_tile", align_bytes=64)
         gate_rows = keep.tile([P, BLOCK], F32, name="gate_rows")
         identity = keep.tile([P, P], F32, name="identity")
-        warm = keep.tile([P, 2], F32, name="warm")
-        nc.gpsimd.memset(w2_plane[:].bitcast(I32), 0)
+        nc.gpsimd.memset(w2_scale_tile[:].bitcast(I32), 0)
         nc.gpsimd.memset(gate_rows[:], 0.0)
-        nc.gpsimd.memset(warm[:], 0.0)
         make_identity(nc, identity[:])
-        nc.scalar.dma_start(w2_codes[:].bitcast(I32), w2_words[0].rearrange("p n t -> p (n t)").bitcast(I32))
-        for q in range(4):
-            nc.scalar.dma_start(
-                w2_plane[32 * q : 32 * q + 4, :].bitcast(I32), w2_scales[0, 4 * q : 4 * q + 4, :].bitcast(I32)
-            )
-        nc.scalar.dma_start(gate_rows[0:blocks, :], gate[0:1, :].rearrange("o (c q) -> (o c) q", q=BLOCK))
-        nc.scalar.activation(warm[:, 1:2], warm[:, 0:1], ACT.Silu)
+        nc.scalar.dma_start(gate_rows[0:BLOCKS, :], gate[0:1, :].rearrange("o (c q) -> (o c) q", q=BLOCK))
 
         x_rows = xT.rearrange("(p j) c -> p j c", j=PACK)
-        x_cuts = ([0, 1024, 2048], [0, 512, 1024, 1536, 2048])
-        x_raw = []
-        for u in range(2):
-            for lo, hi in zip(x_cuts[u][:-1], x_cuts[u][1:]):
-                raw = keep.tile([P, 2, hi - lo], F32, name="x_raw_%d_%d" % (u, lo))
-                nc.sync.dma_start(raw[:], x_rows[:, 2 * u : 2 * u + 2, lo:hi])
-                x_raw.append((u, lo, hi, raw))
+        x_raw = {}
+        for u, loads in enumerate(X_LOADS):
+            for first, last, scalar_share in loads:
+                x_raw[u, first] = keep.tile([P, 2, last - first], F32, name="x_raw_%d_%d" % (u, first))
+                nc.sync.dma_start(x_raw[u, first][:], x_rows[:, 2 * u : 2 * u + 2, first:last])
+            if u == 0:
+                nc.sync.dma_start(offsets[:], offs)
         w_raw = []
         for i, w in enumerate((w1, w3)):
-            for half in range(2):
-                raw = keep.tile([P, PACK, H // 2], F32, name="w_raw_%d_%d" % (i, half))
-                nc.sync.dma_start(
-                    raw[:], w.rearrange("(p j) c -> p j c", j=PACK)[:, :, half * (H // 2) : (half + 1) * (H // 2)]
-                )
-                w_raw.append(raw)
+            w_raw.append(keep.tile([P, PACK, H], F32, name="w_raw_%d" % i))
+            nc.sync.dma_start(w_raw[i][:], w.rearrange("(p j) c -> p j c", j=PACK))
         window = keep.tile([P, T], F32, name="window")
         nc.sync.dma_start(window[:], res)
+        nc.sync.dma_start(w2_code_tile[:].bitcast(I32), w2_words[0].rearrange("p n t -> p (n t)").bitcast(I32))
+        for q in range(4):
+            nc.sync.dma_start(
+                w2_scale_tile[32 * q : 32 * q + 4, :].bitcast(I32), w2_scales[0, 4 * q : 4 * q + 4, :].bitcast(I32)
+            )
+        w2_q = (w2_code_tile, w2_scale_tile)
 
-        gate_bank = psum.tile([P, P], F32, name="back", tag="back")
+        gate_bank = bank(RING - 1, [P, P])
         nc.tensor.transpose(gate_bank[:], gate_rows[:], identity[:])
-        gate_cols = keep.tile([P, blocks], F32, name="gate_cols")
-        nc.scalar.copy(gate_cols[:], gate_bank[:, 0:blocks])
+        gate_cols = keep.tile([P, BLOCKS], F32, name="gate_cols")
+        nc.scalar.copy(gate_cols[:], gate_bank[:, 0:BLOCKS])
 
         pairs = [keep.tile([P, T], U32, name="pairs_%d" % u) for u in range(2)]
+        picked = [keep.tile([P, HALF * PACK], BF16, name="picked_%d" % g, align_bytes=64) for g in range(2)]
+        for u, loads in enumerate(X_LOADS):
+            for first, last, scalar_share in loads:
+                for engine, lo, hi in ((nc.scalar, 0, scalar_share), (nc.vector, scalar_share, last - first)):
+                    if lo < hi:
+                        dst = pairs[u][:, first + lo : first + hi].bitcast(BF16).rearrange("p (c e) -> p c e", e=2)
+                        copy(engine, dst, x_raw[u, first][:, :, lo:hi].rearrange("p e c -> p c e"))
+            for g in range(2):
+                words = picked[g][:].bitcast(U32).rearrange("p (n u) -> p n u", u=2)
+                nc.vector.tensor_copy(words[:, :, u], pairs[u][:].indirect(entries(g)))
 
-        def round_pairs(engine, piece, a, b):
-            u, lo, hi, raw = piece
-            dst = pairs[u][:, lo + a : lo + b].bitcast(BF16).rearrange("p (c e) -> p c e", e=2)
-            src = raw[:, :, a:b].rearrange("p e c -> p c e")
-            if engine is nc.scalar:
-                nc.scalar.copy(dst, src)
-            else:
-                nc.vector.tensor_copy(dst, src)
+        def round_weights(i, engine):
+            tag = "w_rounded_%d" % i
+            rounded = keep.tile([P, H * PACK], BF16, name=tag, tag=tag, align_bytes=64)
+            copy(
+                engine,
+                rounded[:].rearrange("p (t m j) -> p m j t", t=PACK, j=PACK),
+                w_raw[i][:].rearrange("p j (m t) -> p m j t", t=PACK),
+            )
+            return rounded
 
-        picked = [keep.tile([P, GROUP * PACK], BF16, name="picked_%d" % g, align_bytes=64) for g in range(groups)]
+        w1_rounded = round_weights(0, nc.scalar)
+        x_q = [quantize("x_0", picked[0][:])]
+        w3_rounded = round_weights(1, nc.vector)
+        w_q = [quantize("w1", w1_rounded[:]), quantize("w3", w3_rounded[:])]
+        x_q.append(quantize("x_1", picked[1][:], tag="w_rounded_1"))
 
-        def pick(u, g):
-            words = picked[g][:].bitcast(U32).rearrange("p (n u) -> p n u", u=2)
-            nc.vector.tensor_copy(words[:, :, u], pairs[u][:].indirect(entries(g)))
-
-        def quantize(name, grouped, width, tag=None):
-            codes = keep.tile([P, width], U32, name=name + "_codes", tag=tag or name + "_codes", align_bytes=64)
-            plane = keep.tile([P, width], U8, name=name + "_plane", align_bytes=64)
-            nc.vector.quantize_mx(out=codes[:].bitcast(FP8X4), scales=plane[:], in_=grouped)
-            return codes, plane
-
-        round_pairs(nc.vector, x_raw[0], 0, 1024)
-        round_pairs(nc.vector, x_raw[1], 0, 672)
-        round_pairs(nc.scalar, x_raw[1], 672, 1024)
-        for g in range(groups):
-            pick(0, g)
-        for piece in x_raw[2:5]:
-            round_pairs(nc.scalar, piece, 0, 512)
-        round_pairs(nc.vector, x_raw[5], 0, 352)
-        round_pairs(nc.scalar, x_raw[5], 352, 512)
-
-        w_grouped = [keep.tile([P, H * PACK], BF16, name="w_grouped_%d" % i, tag="w_grouped_%d" % i, align_bytes=64) for i in range(2)]
-
-        def round_weights(engine, i, half):
-            dst = w_grouped[i][:].rearrange("p (t m j) -> p m j t", t=PACK, j=PACK)[:, half * 64 : (half + 1) * 64]
-            src = w_raw[2 * i + half][:].rearrange("p j (m t) -> p m j t", t=PACK)
-            if engine is nc.scalar:
-                nc.scalar.copy(dst, src)
-            else:
-                nc.vector.tensor_copy(dst, src)
-
-        round_weights(nc.scalar, 0, 0)
-        round_weights(nc.scalar, 0, 1)
-        round_weights(nc.scalar, 1, 0)
-        pick(1, 0)
-        pick(1, 1)
-        x_q = [quantize("x_0", picked[0][:], GROUP)]
-        w1_q = quantize("w1", w_grouped[0][:], H)
-        round_weights(nc.vector, 1, 1)
-        w3_q = quantize("w3", w_grouped[1][:], H)
-        x_q.append(quantize("x_1", picked[1][:], GROUP, tag="w_grouped_1"))
-
-        def first_layer(name, w_q, c):
-            bank = psum.tile([P, PACK, BLOCK], F32, name=name, tag=name, bufs=3)
-            codes, plane = x_q[c * BLOCK // GROUP]
-            cols = slice(c * BLOCK % GROUP, c * BLOCK % GROUP + BLOCK)
+        def first_layer(i, c):
+            acc = bank(RING * i + c % RING, [P, PACK, BLOCK])
+            g, place = divmod(c, BLOCKS_PER_HALF)
+            tokens = slice(place * BLOCK, (place + 1) * BLOCK)
             for t in range(PACK):
-                w_cols = slice(t * P, (t + 1) * P)
-                nc.tensor.matmul_mx(
-                    out=bank[:, t, :],
-                    lhsT=w_q[0][:, w_cols].bitcast(FP8X4),
-                    lhsT_scale=w_q[1][:, w_cols],
-                    rhs=codes[:, cols].bitcast(FP8X4),
-                    rhs_scale=plane[:, cols],
-                    start=True,
-                    stop=True,
-                )
-            return bank
+                product(acc[:, t, :], w_q[i], slice(t * P, (t + 1) * P), x_q[g], tokens)
+            return acc[:].rearrange("p t n -> p n t")
 
-        h_grouped = [keep.tile([P, GROUP * PACK], BF16, name="h_grouped_%d" % g, align_bytes=64) for g in range(groups)]
+        h_rounded = [
+            keep.tile([P, HALF * PACK], BF16, name="h_rounded_%d" % g, tag="h_rounded_%d" % g, align_bytes=64)
+            for g in range(2)
+        ]
 
         def hidden(c):
-            a_bank = first_layer("a_bank", w1_q, c)
-            silu_a = ring.tile([P, BLOCK, PACK], F32, name="silu_a")
-            nc.scalar.activation(silu_a[:], a_bank[:].rearrange("p t n -> p n t"), ACT.Silu)
-            b_bank = first_layer("b_bank", w3_q, c)
-            g, first = divmod(c * BLOCK, GROUP)
-            dst = h_grouped[g][:, first * PACK : (first + BLOCK) * PACK].rearrange("p (n t) -> p n t", t=PACK)
-            nc.vector.tensor_tensor(dst, b_bank[:].rearrange("p t n -> p n t"), silu_a[:], ALU.mult)
+            silu = keep.tile([P, BLOCK, PACK], F32, name="silu_%d" % c, tag="silu_%d" % c, align_bytes=64)
+            nc.scalar.activation(silu[:], first_layer(0, c), ACT.Silu)
+            linear = first_layer(1, c)
+            g, place = divmod(c, BLOCKS_PER_HALF)
+            dst = h_rounded[g][:].rearrange("p (c n t) -> p c n t", n=BLOCK, t=PACK)[:, place]
+            if place == GPSIMD_PLACE:
+                linear_copy = keep.tile([P, BLOCK, PACK], F32, name="linear_copy_%d" % g)
+                nc.scalar.copy(linear_copy[:], linear)
+                nc.gpsimd.tensor_tensor(dst, linear_copy[:], silu[:], ALU.mult)
+            else:
+                nc.vector.tensor_tensor(dst, linear, silu[:], ALU.mult)
 
-        gated = [keep.tile([P, GROUP], F32, name="gated_%d" % g) for g in range(groups)]
+        def look_up_res(g, tag):
+            old = keep.tile([P, HALF], F32, name="old_%d" % g, tag=tag, align_bytes=64)
+            nc.vector.tensor_copy(old[:], window[:].indirect(entries(g)))
+            return old
 
         def second_layer(g):
-            codes, plane = quantize("h_%d" % g, h_grouped[g][:], GROUP)
-            per = GROUP // BLOCK
-            y_bank = psum.tile([P, per, N], F32, name="y_bank", tag="y_bank")
-            for b in range(per):
-                cols = slice(b * BLOCK, (b + 1) * BLOCK)
-                nc.tensor.matmul_mx(
-                    out=y_bank[:, b, :],
-                    lhsT=codes[:, cols].bitcast(FP8X4),
-                    lhsT_scale=plane[:, cols],
-                    rhs=w2_codes[:].bitcast(FP8X4),
-                    rhs_scale=w2_plane[:],
-                    start=True,
-                    stop=True,
+            y_bank = bank(RING - 1 - g, [P, BLOCKS_PER_HALF, N])
+            for place in range(BLOCKS_PER_HALF):
+                tokens = slice(place * BLOCK, (place + 1) * BLOCK)
+                product(y_bank[:, place, :], h_q[g], tokens, w2_q, slice(0, N))
+            y_gated = keep.tile([P, BLOCKS_PER_HALF, N], F32, name="y_gated_%d" % g)
+            for place in range(BLOCKS_PER_HALF):
+                c = g * BLOCKS_PER_HALF + place
+                nc.scalar.activation(
+                    y_gated[:, place, :], y_bank[:, place, :], ACT.Copy, scale=gate_cols[:, c : c + 1]
                 )
-            y_tok = ring.tile([P, per, N], F32, name="y_tok")
-            for b in range(per):
-                c = g * per + b
-                nc.scalar.activation(y_tok[:, b, :], y_bank[:, b, :], ACT.Copy, scale=gate_cols[:, c : c + 1])
-            back = psum.tile([P, GROUP], F32, name="back", tag="back")
-            for b in range(per):
-                nc.tensor.transpose(back[:, b * BLOCK : (b + 1) * BLOCK], y_tok[:, b, :], identity[:])
-            nc.scalar.copy(gated[g][:], back[:])
+            turned = bank(RING - 2 - g, [P, HALF])
+            for place in range(BLOCKS_PER_HALF):
+                tokens = slice(place * BLOCK, (place + 1) * BLOCK)
+                nc.tensor.transpose(turned[:, tokens], y_gated[:, place, :], identity[:])
+            update = keep.tile([P, HALF], F32, name="update_%d" % g)
+            nc.scalar.copy(update[:], turned[:])
+            return update
 
-        per = GROUP // BLOCK
-        for c in range(blocks):
+        hidden(0)
+        old = [look_up_res(0, "silu_0")]
+        for c in range(1, BLOCKS_PER_HALF + 1):
             hidden(c)
-            if c >= per and c % per == 0:
-                second_layer(c // per - 1)
-        second_layer(groups - 1)
-        old = h_grouped[groups - 1][:].bitcast(F32)
-        nc.vector.tensor_copy(old, window[:].indirect(offsets[:]))
+        h_q = [quantize("h_0", h_rounded[0][:])]
+        for c in range(BLOCKS_PER_HALF + 1, BLOCKS):
+            hidden(c)
+        h_q.append(quantize("h_1", h_rounded[1][:]))
+        old.append(look_up_res(1, "h_rounded_1"))
+        updates = [second_layer(g) for g in range(2)]
 
-        for g in range(groups):
-            nc.vector.tensor_tensor(
-                window[:].indirect(entries(g)), gated[g][:], old[:, g * GROUP : (g + 1) * GROUP], ALU.add
-            )
+        for g in range(2):
+            nc.vector.tensor_tensor(window[:].indirect(entries(g)), updates[g][:], old[g][:], ALU.add)
         nc.sync.dma_start(out, window[:])

from contextlib import ExitStack

import concourse.mybir as mybir
from concourse.masks import make_identity

K, T, S, H, N = 512, 2048, 1024, 512, 128
FLOPS = 2 * (2 * K * H * S) + 2 * H * N * S
BYTES = 4 * (K * T + S + 2 * N * T + 2 * K * H) + H * N + (H // 32) * N + 2 * 128 * (S // 16)

F32 = mybir.dt.float32
BF16 = mybir.dt.bfloat16
U32 = mybir.dt.uint32
U16 = mybir.dt.uint16
U8 = mybir.dt.uint8
I32 = mybir.dt.int32
FP8X4 = mybir.dt.float8_e4m3fn_x4
ACT = mybir.ActivationFunctionType
ALU = mybir.AluOpType

P = 128
PACK = 4
LANES = 16
BLOCK = 128
HALF = 512
BLOCKS = S // BLOCK
BLOCKS_PER_HALF = HALF // BLOCK
GPSIMD_PLACE = 1
RING = 4

X_LOADS = (
    ((0, 1024, 0), (1024, 2048, 352)),
    ((0, 768, 768), (768, 1536, 416), (1536, 2048, 160)),
)


def tile_picked_modres_glusilu_l_kernel(
    tc, xT, gate, res, w1, w3, w2_words, w2_scales, offs, out
):
    nc = tc.nc

    with ExitStack() as ctx:
        keep = ctx.enter_context(tc.tile_pool(name="keep", bufs=1))
        psum = ctx.enter_context(tc.psum_pool(name="psum", bufs=1))

        def copy(engine, dst, src):
            if engine is nc.scalar:
                nc.scalar.copy(dst, src)
            else:
                nc.vector.tensor_copy(dst, src)

        def quantize(name, values, tag=""):
            width = values.shape[1] // PACK
            codes = keep.tile([P, width], U32, name=name + "_codes", tag=tag or name + "_codes", align_bytes=64)
            scales = keep.tile([P, width], U8, name=name + "_scales", align_bytes=64)
            nc.vector.quantize_mx(out=codes[:].bitcast(FP8X4), scales=scales[:], in_=values)
            return codes, scales

        def product(dst, stationary, stationary_cols, moving, moving_cols):
            nc.tensor.matmul_mx(
                out=dst,
                lhsT=stationary[0][:, stationary_cols].bitcast(FP8X4),
                lhsT_scale=stationary[1][:, stationary_cols],
                rhs=moving[0][:, moving_cols].bitcast(FP8X4),
                rhs_scale=moving[1][:, moving_cols],
                start=True,
                stop=True,
            )

        def bank(number, shape):
            return psum.tile(shape, F32, name="bank_%d" % number, tag="bank_%d" % number)

        offsets = keep.tile([P, S // LANES], U16, name="offsets")

        def entries(g):
            return offsets[:, g * HALF // LANES : (g + 1) * HALF // LANES]

        w2_code_tile = keep.tile([P, N], U32, name="w2_code_tile", align_bytes=64)
        w2_scale_tile = keep.tile([P, N], U8, name="w2_scale_tile", align_bytes=64)
        gate_rows = keep.tile([P, BLOCK], F32, name="gate_rows")
        identity = keep.tile([P, P], F32, name="identity")
        nc.gpsimd.memset(w2_scale_tile[:].bitcast(I32), 0)
        nc.gpsimd.memset(gate_rows[:], 0.0)
        make_identity(nc, identity[:])
        nc.scalar.dma_start(gate_rows[0:BLOCKS, :], gate[0:1, :].rearrange("o (c q) -> (o c) q", q=BLOCK))

        x_rows = xT.rearrange("(p j) c -> p j c", j=PACK)
        x_raw = {}
        for u, loads in enumerate(X_LOADS):
            for first, last, scalar_share in loads:
                x_raw[u, first] = keep.tile([P, 2, last - first], F32, name="x_raw_%d_%d" % (u, first))
                nc.sync.dma_start(x_raw[u, first][:], x_rows[:, 2 * u : 2 * u + 2, first:last])
            if u == 0:
                nc.sync.dma_start(offsets[:], offs)
        w_raw = []
        for i, w in enumerate((w1, w3)):
            w_raw.append(keep.tile([P, PACK, H], F32, name="w_raw_%d" % i))
            nc.sync.dma_start(w_raw[i][:], w.rearrange("(p j) c -> p j c", j=PACK))
        window = keep.tile([P, T], F32, name="window")
        nc.sync.dma_start(window[:], res)
        nc.sync.dma_start(w2_code_tile[:].bitcast(I32), w2_words[0].rearrange("p n t -> p (n t)").bitcast(I32))
        for q in range(4):
            nc.sync.dma_start(
                w2_scale_tile[32 * q : 32 * q + 4, :].bitcast(I32), w2_scales[0, 4 * q : 4 * q + 4, :].bitcast(I32)
            )
        w2_q = (w2_code_tile, w2_scale_tile)

        gate_bank = bank(RING - 1, [P, P])
        nc.tensor.transpose(gate_bank[:], gate_rows[:], identity[:])
        gate_cols = keep.tile([P, BLOCKS], F32, name="gate_cols")
        nc.scalar.copy(gate_cols[:], gate_bank[:, 0:BLOCKS])

        pairs = [keep.tile([P, T], U32, name="pairs_%d" % u) for u in range(2)]
        picked = [keep.tile([P, HALF * PACK], BF16, name="picked_%d" % g, align_bytes=64) for g in range(2)]
        for u, loads in enumerate(X_LOADS):
            for first, last, scalar_share in loads:
                for engine, lo, hi in ((nc.scalar, 0, scalar_share), (nc.vector, scalar_share, last - first)):
                    if lo < hi:
                        dst = pairs[u][:, first + lo : first + hi].bitcast(BF16).rearrange("p (c e) -> p c e", e=2)
                        copy(engine, dst, x_raw[u, first][:, :, lo:hi].rearrange("p e c -> p c e"))
            for g in range(2):
                words = picked[g][:].bitcast(U32).rearrange("p (n u) -> p n u", u=2)
                nc.vector.tensor_copy(words[:, :, u], pairs[u][:].indirect(entries(g)))

        def round_weights(i, engine):
            tag = "w_rounded_%d" % i
            rounded = keep.tile([P, H * PACK], BF16, name=tag, tag=tag, align_bytes=64)
            copy(
                engine,
                rounded[:].rearrange("p (t m j) -> p m j t", t=PACK, j=PACK),
                w_raw[i][:].rearrange("p j (m t) -> p m j t", t=PACK),
            )
            return rounded

        w1_rounded = round_weights(0, nc.scalar)
        x_q = [quantize("x_0", picked[0][:])]
        w3_rounded = round_weights(1, nc.vector)
        w_q = [quantize("w1", w1_rounded[:]), quantize("w3", w3_rounded[:])]
        x_q.append(quantize("x_1", picked[1][:], tag="w_rounded_1"))

        def first_layer(i, c):
            acc = bank(RING * i + c % RING, [P, PACK, BLOCK])
            g, place = divmod(c, BLOCKS_PER_HALF)
            tokens = slice(place * BLOCK, (place + 1) * BLOCK)
            for t in range(PACK):
                product(acc[:, t, :], w_q[i], slice(t * P, (t + 1) * P), x_q[g], tokens)
            return acc[:].rearrange("p t n -> p n t")

        h_rounded = [
            keep.tile([P, HALF * PACK], BF16, name="h_rounded_%d" % g, tag="h_rounded_%d" % g, align_bytes=64)
            for g in range(2)
        ]

        def hidden(c):
            silu = keep.tile([P, BLOCK, PACK], F32, name="silu_%d" % c, tag="silu_%d" % c, align_bytes=64)
            nc.scalar.activation(silu[:], first_layer(0, c), ACT.Silu)
            linear = first_layer(1, c)
            g, place = divmod(c, BLOCKS_PER_HALF)
            dst = h_rounded[g][:].rearrange("p (c n t) -> p c n t", n=BLOCK, t=PACK)[:, place]
            if place == GPSIMD_PLACE:
                linear_copy = keep.tile([P, BLOCK, PACK], F32, name="linear_copy_%d" % g)
                nc.scalar.copy(linear_copy[:], linear)
                nc.gpsimd.tensor_tensor(dst, linear_copy[:], silu[:], ALU.mult)
            else:
                nc.vector.tensor_tensor(dst, linear, silu[:], ALU.mult)

        def look_up_res(g, tag):
            old = keep.tile([P, HALF], F32, name="old_%d" % g, tag=tag, align_bytes=64)
            nc.vector.tensor_copy(old[:], window[:].indirect(entries(g)))
            return old

        def second_layer(g):
            y_bank = bank(RING - 1 - g, [P, BLOCKS_PER_HALF, N])
            for place in range(BLOCKS_PER_HALF):
                tokens = slice(place * BLOCK, (place + 1) * BLOCK)
                product(y_bank[:, place, :], h_q[g], tokens, w2_q, slice(0, N))
            y_gated = keep.tile([P, BLOCKS_PER_HALF, N], F32, name="y_gated_%d" % g)
            for place in range(BLOCKS_PER_HALF):
                c = g * BLOCKS_PER_HALF + place
                nc.scalar.activation(
                    y_gated[:, place, :], y_bank[:, place, :], ACT.Copy, scale=gate_cols[:, c : c + 1]
                )
            turned = bank(RING - 2 - g, [P, HALF])
            for place in range(BLOCKS_PER_HALF):
                tokens = slice(place * BLOCK, (place + 1) * BLOCK)
                nc.tensor.transpose(turned[:, tokens], y_gated[:, place, :], identity[:])
            update = keep.tile([P, HALF], F32, name="update_%d" % g)
            nc.scalar.copy(update[:], turned[:])
            return update

        hidden(0)
        old = [look_up_res(0, "silu_0")]
        for c in range(1, BLOCKS_PER_HALF + 1):
            hidden(c)
        h_q = [quantize("h_0", h_rounded[0][:])]
        for c in range(BLOCKS_PER_HALF + 1, BLOCKS):
            hidden(c)
        h_q.append(quantize("h_1", h_rounded[1][:]))
        old.append(look_up_res(1, "h_rounded_1"))
        updates = [second_layer(g) for g in range(2)]

        for g in range(2):
            nc.vector.tensor_tensor(window[:].indirect(entries(g)), updates[g][:], old[g][:], ALU.add)
        nc.sync.dma_start(out, window[:])
